import numpy as np
import ml_dtypes


def mxq(x, axis, fmt="e4m3"):
    dtype, down = {"e4m3": (ml_dtypes.float8_e4m3fn, 7), "e5m2": (ml_dtypes.float8_e5m2, 14)}[fmt]
    v = np.moveaxis(np.asarray(x, np.float32).astype(ml_dtypes.bfloat16).astype(np.float64), axis, -1)
    blocks = v.reshape(v.shape[:-1] + (-1, 32))
    amax = np.abs(blocks).max(-1, keepdims=True)
    byte = np.maximum(np.where(amax > 0, np.frexp(amax)[1] - 1 + 127, 0) - down, 1)
    scale = np.exp2(byte - 127.0)
    codes = (blocks / scale).astype(np.float32).astype(dtype).astype(np.float64)
    return np.moveaxis((codes * scale).reshape(v.shape), -1, axis)


WIDE = False


def mx_kscale(k):
    if not WIDE:
        return np.ones(k)
    levels = np.array([10, -10, 5, -5, 0])
    if k % 512:
        return np.exp2(np.random.permutation(np.resize(levels, k // 32))).repeat(32)
    a = np.empty((k // 512, 16))
    for p in range(k // 512):
        a[p, :8] = np.random.permutation(np.resize(levels, 8))
        for g in range(8):
            far = levels[np.abs(levels - a[p, g]) >= 10]
            a[p, g + 8] = far[np.random.randint(len(far))]
    return np.exp2(a.ravel()).repeat(32)


def f64(x):
    return np.asarray(x).astype(np.float64)


def striped(idx):
    return np.tile(idx.reshape(-1, 16).T, (8, 1)).astype(np.uint16)


def unstriped(offs):
    return offs[:16].T.reshape(-1).astype(np.int64)


def relu(v):
    return np.maximum(v, 0.0)


K, T, D, S, V, N = 512, 512, 4, 512, 128, 256


def setup_inputs():
    n = np.random.standard_normal
    s = mx_kscale(K)[:, None]
    return {
        "xT": (n((K, T)) * s).astype(np.float32),
        "w": (n((D, K, N)) / np.sqrt(D * K) / s[None]).astype(np.float32),
        "b": (0.3 * n((N, 1))).astype(np.float32),
        "gate": np.tile(np.random.uniform(0.2, 1.0, S), (N, 1)).astype(np.float32),
        "offs": striped(np.random.permutation(T)[:S]),
    }


def reference(xT, w, b, gate, offs):
    idx = unstriped(offs)
    xq = mxq(f64(xT)[:, idx], 0, "e4m3")
    wq = mxq(f64(w), 1, "e4m3")
    y = sum(wq[d].T @ xq[:, d * V:(d + 1) * V] for d in range(D))
    y = relu(y + f64(b))
    out = np.zeros((N, T))
    out[:, idx] = f64(gate) * np.tile(y, (1, D))
    return out

@@ -1,0 +1,150 @@
+from contextlib import ExitStack
+
+import concourse.mybir as mybir
+
+K, T, D, V, N = 512, 512, 4, 128, 256
+P = 128
+J = 4
+MB = N // P
+XC = 256
+FLOPS = 2 * D * K * V * N
+
+F32 = mybir.dt.float32
+BF16 = mybir.dt.bfloat16
+U32 = mybir.dt.uint32
+U16 = mybir.dt.uint16
+U8 = mybir.dt.uint8
+FP8X4 = mybir.dt.float8_e4m3fn_x4
+RELU = mybir.ActivationFunctionType.Relu
+MULT = mybir.AluOpType.mult
+
+
+def tile_picked_tome_lin_relu_sub_e_kernel(tc, xT, w, b, gate, offs, out):
+    nc = tc.nc
+    with ExitStack() as ctx:
+        lists = ctx.enter_context(tc.tile_pool(name="lists", bufs=1))
+        keep = ctx.enter_context(tc.tile_pool(name="keep", bufs=1))
+        psum = ctx.enter_context(tc.psum_pool(name="psum", bufs=1))
+
+        offsets = lists.tile([P, T // 16], U16, name="offsets")
+
+        x_raw = [keep.tile([P, J, XC], F32, name=f"x_raw{c}") for c in range(T // XC)]
+        x_bf = [keep.tile([P, XC, J], BF16, name=f"x_bf{c}", align_bytes=64) for c in range(T // XC)]
+        x_codes = keep.tile([P, T], U32, name="x_codes", align_bytes=64)
+        x_scales = keep.tile([P, T], U8, name="x_scales", align_bytes=64)
+        g_codes = keep.tile([P, T], U32, name="g_codes", align_bytes=64)
+        g_scales = keep.tile([P, T], U8, name="g_scales", align_bytes=64)
+        w_raw = [[keep.tile([P, J, P], F32, name=f"w_raw{m}_{d}") for d in range(D)] for m in range(MB)]
+        w_bf = [keep.tile([P, D, P, J], BF16, name=f"w_bf{m}", align_bytes=64) for m in range(MB)]
+        w_codes = [keep.tile([P, D, P], U32, name=f"w_codes{m}", align_bytes=64) for m in range(MB)]
+        w_scales = [keep.tile([P, D, P], U8, name=f"w_scales{m}", align_bytes=64) for m in range(MB)]
+        bias = [keep.tile([P, 1], F32, name=f"bias{m}") for m in range(MB)]
+        gates = [keep.tile([P, T], F32, name=f"gates{m}") for m in range(MB)]
+        y = [keep.tile([P, 2 * V], F32, name=f"y{m}") for m in range(MB)]
+        spread = [keep.tile([P, T], F32, name=f"spread{m}") for m in range(MB)]
+        warm = keep.tile([P, 2], F32, name="warm")
+        acc = [psum.tile([P, V], F32, name=f"acc{m}") for m in range(MB)]
+
+        nc.gpsimd.memset(warm[:, 0:1], 0.0)
+        nc.scalar.activation(warm[:, 1:2], warm[:, 0:1], RELU)
+        nc.gpsimd.memset(x_scales[:], 0)
+
+        x_view = xT.rearrange("(p j) t -> p j t", j=J)
+
+        def load_w(m, d):
+            src = w[d].rearrange("(p j) n -> p j n", j=J)[:, :, m * P : (m + 1) * P]
+            nc.sync.dma_start(out=w_raw[m][d][:], in_=src)
+
+        def group(engine_copy, dst, src):
+            engine_copy(
+                out=dst.rearrange("p (c i) t -> p c t i", i=4),
+                in_=src.rearrange("p t (c i) -> p c t i", i=4),
+            )
+
+        nc.sync.dma_start(out=x_raw[0][:], in_=x_view[:, :, 0:XC])
+        nc.sync.dma_start(offsets[:], offs)
+        nc.sync.dma_start(out=x_raw[1][:], in_=x_view[:, :, XC : 2 * XC])
+        for d in range(D):
+            load_w(0, d)
+        for m in range(MB):
+            nc.sync.dma_start(out=bias[m][:], in_=b[m * P : (m + 1) * P, :])
+        load_w(1, 0)
+        load_w(1, 1)
+        nc.sync.dma_start(out=gates[0][:], in_=gate[0:P, :])
+        load_w(1, 2)
+        load_w(1, 3)
+        nc.sync.dma_start(out=gates[1][:], in_=gate[P : 2 * P, :])
+
+        for c in range(T // XC):
+            s = XC - 96
+            group(nc.vector.tensor_copy, x_bf[c][:, 0:s, :], x_raw[c][:, :, 0:s])
+            group(nc.scalar.copy, x_bf[c][:, s:XC, :], x_raw[c][:, :, s:XC])
+            cols = slice(c * XC, (c + 1) * XC)
+            nc.vector.quantize_mx(
+                out=x_codes[:, cols].bitcast(FP8X4),
+                scales=x_scales[:, cols],
+                in_=x_bf[c][:].rearrange("p t j -> p (t j)"),
+            )
+
+        def gather(dst, src, h):
+            nc.vector.tensor_copy(dst[:, h * 256 : (h + 1) * 256], src[:].indirect(offsets[:, h * 16 : (h + 1) * 16]))
+
+        def quantize_w(m, a, e):
+            nc.vector.quantize_mx(
+                out=w_codes[m][:, a:e, :].rearrange("p d n -> p (d n)").bitcast(FP8X4),
+                scales=w_scales[m][:, a:e, :].rearrange("p d n -> p (d n)"),
+                in_=w_bf[m][:, a:e, :, :].rearrange("p d n j -> p (d n j)"),
+            )
+
+        def multiply(m, d):
+            nc.tensor.matmul_mx(
+                out=acc[m][:],
+                lhsT=w_codes[m][:, d, :].bitcast(FP8X4),
+                lhsT_scale=w_scales[m][:, d, :],
+                rhs=g_codes[:, d * V : (d + 1) * V].bitcast(FP8X4),
+                rhs_scale=g_scales[:, d * V : (d + 1) * V],
+                start=(d == 0),
+                stop=(d == D - 1),
+            )
+
+        def finish(m):
+            for r in range(2):
+                nc.scalar.activation(y[m][:, r * V : (r + 1) * V], acc[m][:], RELU, bias=bias[m][:])
+
+        def scatter(m, a, e):
+            nc.vector.tensor_tensor(
+                spread[m][:].indirect(offsets[:, a * 8 : e * 8]),
+                y[m][:, 0 : (e - a) * V],
+                gates[m][:, a * V : e * V],
+                MULT,
+            )
+
+        for d in range(D):
+            group(nc.scalar.copy, w_bf[0][:, d, :, :], w_raw[0][d][:])
+        gather(g_codes, x_codes, 0)
+        gather(g_scales, x_scales, 0)
+        gather(g_codes, x_codes, 1)
+        quantize_w(0, 0, 2)
+        multiply(0, 0)
+        multiply(0, 1)
+        for d in range(2):
+            group(nc.scalar.copy, w_bf[1][:, d, :, :], w_raw[1][d][:])
+        gather(g_scales, x_scales, 1)
+        quantize_w(0, 2, 4)
+        multiply(0, 2)
+        multiply(0, 3)
+        quantize_w(1, 0, 2)
+        finish(0)
+        for d in range(2, D):
+            group(nc.scalar.copy, w_bf[1][:, d, :, :], w_raw[1][d][:])
+        scatter(0, 0, 2)
+        scatter(0, 2, 3)
+        quantize_w(1, 2, 4)
+        for d in range(D):
+            multiply(1, d)
+        finish(1)
+        scatter(0, 3, 4)
+        nc.sync.dma_start(out=out[0:P, :], in_=spread[0][:])
+        scatter(1, 0, 2)
+        scatter(1, 2, 4)
+        nc.sync.dma_start(out=out[P : 2 * P, :], in_=spread[1][:])

@@ -6,7 +6,7 @@ K, T, D, V, N = 512, 512, 4, 128, 256
 P = 128
 J = 4
 MB = N // P
-XC = 256
+XV = 320
 FLOPS = 2 * D * K * V * N
 
 F32 = mybir.dt.float32
@@ -28,17 +28,17 @@ def tile_picked_tome_lin_relu_sub_e_kernel(tc, xT, w, b, gate, offs, out):
 
         offsets = lists.tile([P, T // 16], U16, name="offsets")
 
-        x_raw = [keep.tile([P, J, XC], F32, name=f"x_raw{c}") for c in range(T // XC)]
-        x_bf = [keep.tile([P, XC, J], BF16, name=f"x_bf{c}", align_bytes=64) for c in range(T // XC)]
+        x_raw = [keep.tile([P, 2, T], F32, name=f"x_raw{u}") for u in range(2)]
+        x_bf = keep.tile([P, T, J], BF16, name="x_bf", align_bytes=64)
         x_codes = keep.tile([P, T], U32, name="x_codes", align_bytes=64)
         x_scales = keep.tile([P, T], U8, name="x_scales", align_bytes=64)
         g_codes = keep.tile([P, T], U32, name="g_codes", align_bytes=64)
         g_scales = keep.tile([P, T], U8, name="g_scales", align_bytes=64)
-        w_raw = [[keep.tile([P, J, P], F32, name=f"w_raw{m}_{d}") for d in range(D)] for m in range(MB)]
+        w_raw = [keep.tile([P, J, N], F32, name=f"w_raw{d}") for d in range(D)]
         w_bf = [keep.tile([P, D, P, J], BF16, name=f"w_bf{m}", align_bytes=64) for m in range(MB)]
         w_codes = [keep.tile([P, D, P], U32, name=f"w_codes{m}", align_bytes=64) for m in range(MB)]
         w_scales = [keep.tile([P, D, P], U8, name=f"w_scales{m}", align_bytes=64) for m in range(MB)]
-        bias = [keep.tile([P, 1], F32, name=f"bias{m}") for m in range(MB)]
+        bias = keep.tile([P, MB], F32, name="bias")
         gates = [keep.tile([P, T], F32, name=f"gates{m}") for m in range(MB)]
         y = [keep.tile([P, 2 * V], F32, name=f"y{m}") for m in range(MB)]
         spread = [keep.tile([P, T], F32, name=f"spread{m}") for m in range(MB)]
@@ -51,9 +51,6 @@ def tile_picked_tome_lin_relu_sub_e_kernel(tc, xT, w, b, gate, offs, out):
 
         x_view = xT.rearrange("(p j) t -> p j t", j=J)
 
-        def load_w(m, d):
-            src = w[d].rearrange("(p j) n -> p j n", j=J)[:, :, m * P : (m + 1) * P]
-            nc.sync.dma_start(out=w_raw[m][d][:], in_=src)
 
         def group(engine_copy, dst, src):
             engine_copy(
@@ -61,29 +58,25 @@ def tile_picked_tome_lin_relu_sub_e_kernel(tc, xT, w, b, gate, offs, out):
                 in_=src.rearrange("p t (c i) -> p c t i", i=4),
             )
 
-        nc.sync.dma_start(out=x_raw[0][:], in_=x_view[:, :, 0:XC])
+        nc.sync.dma_start(out=x_raw[0][:], in_=x_view[:, 0:2, :])
+        nc.sync.dma_start(out=x_raw[1][:], in_=x_view[:, 2:4, :])
         nc.sync.dma_start(offsets[:], offs)
-        nc.sync.dma_start(out=x_raw[1][:], in_=x_view[:, :, XC : 2 * XC])
         for d in range(D):
-            load_w(0, d)
-        for m in range(MB):
-            nc.sync.dma_start(out=bias[m][:], in_=b[m * P : (m + 1) * P, :])
-        load_w(1, 0)
-        load_w(1, 1)
+            nc.sync.dma_start(out=w_raw[d][:], in_=w[d].rearrange("(p j) n -> p j n", j=J))
+        nc.sync.dma_start(out=bias[:], in_=b.rearrange("(m p) o -> p (m o)", p=P))
         nc.sync.dma_start(out=gates[0][:], in_=gate[0:P, :])
-        load_w(1, 2)
-        load_w(1, 3)
         nc.sync.dma_start(out=gates[1][:], in_=gate[P : 2 * P, :])
 
-        for c in range(T // XC):
-            s = XC - 96
-            group(nc.vector.tensor_copy, x_bf[c][:, 0:s, :], x_raw[c][:, :, 0:s])
-            group(nc.scalar.copy, x_bf[c][:, s:XC, :], x_raw[c][:, :, s:XC])
-            cols = slice(c * XC, (c + 1) * XC)
+        for u in range(2):
+            pair = slice(2 * u, 2 * u + 2)
+            group(nc.vector.tensor_copy, x_bf[:, 0:XV, pair], x_raw[u][:, :, 0:XV])
+            group(nc.scalar.copy, x_bf[:, XV:T, pair], x_raw[u][:, :, XV:T])
+        for h in range(2):
+            cols = slice(h * 256, (h + 1) * 256)
             nc.vector.quantize_mx(
                 out=x_codes[:, cols].bitcast(FP8X4),
                 scales=x_scales[:, cols],
-                in_=x_bf[c][:].rearrange("p t j -> p (t j)"),
+                in_=x_bf[:, cols, :].rearrange("p t j -> p (t j)"),
             )
 
         def gather(dst, src, h):
@@ -107,9 +100,8 @@ def tile_picked_tome_lin_relu_sub_e_kernel(tc, xT, w, b, gate, offs, out):
                 stop=(d == D - 1),
             )
 
-        def finish(m):
-            for r in range(2):
-                nc.scalar.activation(y[m][:, r * V : (r + 1) * V], acc[m][:], RELU, bias=bias[m][:])
+        def finish(m, r):
+            nc.scalar.activation(y[m][:, r * V : (r + 1) * V], acc[m][:], RELU, bias=bias[:, m : m + 1])
 
         def scatter(m, a, e):
             nc.vector.tensor_tensor(
@@ -119,30 +111,34 @@ def tile_picked_tome_lin_relu_sub_e_kernel(tc, xT, w, b, gate, offs, out):
                 MULT,
             )
 
-        for d in range(D):
-            group(nc.scalar.copy, w_bf[0][:, d, :, :], w_raw[0][d][:])
+        def copy_w(engine_copy, m, d):
+            group(engine_copy, w_bf[m][:, d, :, :], w_raw[d][:, :, m * P : (m + 1) * P])
+
+        for m, d in ((0, 0), (1, 0), (0, 1), (1, 1), (0, 2), (1, 2)):
+            copy_w(nc.scalar.copy, m, d)
         gather(g_codes, x_codes, 0)
         gather(g_scales, x_scales, 0)
         gather(g_codes, x_codes, 1)
+        gather(g_scales, x_scales, 1)
         quantize_w(0, 0, 2)
         multiply(0, 0)
         multiply(0, 1)
-        for d in range(2):
-            group(nc.scalar.copy, w_bf[1][:, d, :, :], w_raw[1][d][:])
-        gather(g_scales, x_scales, 1)
-        quantize_w(0, 2, 4)
+        quantize_w(0, 2, 3)
         multiply(0, 2)
+        copy_w(nc.vector.tensor_copy, 0, 3)
+        copy_w(nc.scalar.copy, 1, 3)
+        quantize_w(0, 3, 4)
         multiply(0, 3)
+        finish(0, 0)
+        finish(0, 1)
         quantize_w(1, 0, 2)
-        finish(0)
-        for d in range(2, D):
-            group(nc.scalar.copy, w_bf[1][:, d, :, :], w_raw[1][d][:])
-        scatter(0, 0, 2)
-        scatter(0, 2, 3)
         quantize_w(1, 2, 4)
+        scatter(0, 0, 1)
+        scatter(0, 1, 3)
         for d in range(D):
             multiply(1, d)
-        finish(1)
+        finish(1, 0)
+        finish(1, 1)
         scatter(0, 3, 4)
         nc.sync.dma_start(out=out[0:P, :], in_=spread[0][:])
         scatter(1, 0, 2)

@@ -17,6 +17,7 @@ U8 = mybir.dt.uint8
 FP8X4 = mybir.dt.float8_e4m3fn_x4
 RELU = mybir.ActivationFunctionType.Relu
 MULT = mybir.AluOpType.mult
+ADD = mybir.AluOpType.add
 
 
 def tile_picked_tome_lin_relu_sub_e_kernel(tc, xT, w, b, gate, offs, out):
@@ -34,7 +35,8 @@ def tile_picked_tome_lin_relu_sub_e_kernel(tc, xT, w, b, gate, offs, out):
         x_scales = keep.tile([P, T], U8, name="x_scales", align_bytes=64)
         g_codes = keep.tile([P, T], U32, name="g_codes", align_bytes=64)
         g_scales = keep.tile([P, T], U8, name="g_scales", align_bytes=64)
-        w_raw = [keep.tile([P, J, N], F32, name=f"w_raw{d}") for d in range(D)]
+        w_raw = [keep.tile([P, J, N], F32, name=f"w_raw{d}") for d in range(D - 1)]
+        w_last = [keep.tile([P, J, P], F32, name=f"w_last{m}") for m in range(MB)]
         w_bf = [keep.tile([P, D, P, J], BF16, name=f"w_bf{m}", align_bytes=64) for m in range(MB)]
         w_codes = [keep.tile([P, D, P], U32, name=f"w_codes{m}", align_bytes=64) for m in range(MB)]
         w_scales = [keep.tile([P, D, P], U8, name=f"w_scales{m}", align_bytes=64) for m in range(MB)]
@@ -62,7 +64,13 @@ def tile_picked_tome_lin_relu_sub_e_kernel(tc, xT, w, b, gate, offs, out):
         nc.sync.dma_start(out=x_raw[1][:], in_=x_view[:, 2:4, :])
         nc.sync.dma_start(offsets[:], offs)
         for d in range(D):
-            nc.sync.dma_start(out=w_raw[d][:], in_=w[d].rearrange("(p j) n -> p j n", j=J))
+            w_view = w[d].rearrange("(p j) n -> p j n", j=J)
+            if d < D - 1:
+                nc.sync.dma_start(out=w_raw[d][:], in_=w_view)
+            else:
+                for m in range(MB):
+                    cols = slice(m * P, (m + 1) * P)
+                    nc.sync.dma_start(out=w_last[m][:], in_=w_view[:, :, cols])
         nc.sync.dma_start(out=bias[:], in_=b.rearrange("(m p) o -> p (m o)", p=P))
         nc.sync.dma_start(out=gates[0][:], in_=gate[0:P, :])
         nc.sync.dma_start(out=gates[1][:], in_=gate[P : 2 * P, :])
@@ -112,20 +120,27 @@ def tile_picked_tome_lin_relu_sub_e_kernel(tc, xT, w, b, gate, offs, out):
             )
 
         def copy_w(engine_copy, m, d):
-            group(engine_copy, w_bf[m][:, d, :, :], w_raw[d][:, :, m * P : (m + 1) * P])
+            raw = w_raw[d][:, :, m * P : (m + 1) * P] if d < D - 1 else w_last[m][:]
+            group(engine_copy, w_bf[m][:, d, :, :], raw)
 
-        for m, d in ((0, 0), (1, 0), (0, 1), (1, 1), (0, 2), (1, 2)):
-            copy_w(nc.scalar.copy, m, d)
+        def copy_gpsimd(out, in_):
+            nc.gpsimd.tensor_scalar(out, in_, 1.0, 0.0, MULT, ADD)
+
+        for d in range(2):
+            copy_w(nc.scalar.copy, 0, d)
+            copy_w(copy_gpsimd, 1, d)
+        copy_w(nc.scalar.copy, 0, 2)
+        copy_w(nc.scalar.copy, 1, 2)
         gather(g_codes, x_codes, 0)
         gather(g_scales, x_scales, 0)
         gather(g_codes, x_codes, 1)
-        gather(g_scales, x_scales, 1)
         quantize_w(0, 0, 2)
         multiply(0, 0)
         multiply(0, 1)
+        gather(g_scales, x_scales, 1)
+        copy_w(nc.vector.tensor_copy, 0, 3)
         quantize_w(0, 2, 3)
         multiply(0, 2)
-        copy_w(nc.vector.tensor_copy, 0, 3)
         copy_w(nc.scalar.copy, 1, 3)
         quantize_w(0, 3, 4)
         multiply(0, 3)
@@ -139,8 +154,8 @@ def tile_picked_tome_lin_relu_sub_e_kernel(tc, xT, w, b, gate, offs, out):
             multiply(1, d)
         finish(1, 0)
         finish(1, 1)
+        scatter(1, 0, 2)
         scatter(0, 3, 4)
         nc.sync.dma_start(out=out[0:P, :], in_=spread[0][:])
-        scatter(1, 0, 2)
         scatter(1, 2, 4)
         nc.sync.dma_start(out=out[P : 2 * P, :], in_=spread[1][:])

@@ -4,9 +4,14 @@ import concourse.mybir as mybir
 
 K, T, D, V, N = 512, 512, 4, 128, 256
 P = 128
-J = 4
-MB = N // P
-XV = 320
+PACK = 4
+BLOCKS = N // P
+HALF = T // 2
+LIST_STRIPE = 16
+RUN = 4
+
+X_SPLIT = 320
+
 FLOPS = 2 * D * K * V * N
 
 F32 = mybir.dt.float32
@@ -27,135 +32,145 @@ def tile_picked_tome_lin_relu_sub_e_kernel(tc, xT, w, b, gate, offs, out):
         keep = ctx.enter_context(tc.tile_pool(name="keep", bufs=1))
         psum = ctx.enter_context(tc.psum_pool(name="psum", bufs=1))
 
-        offsets = lists.tile([P, T // 16], U16, name="offsets")
+        offsets = lists.tile([P, T // LIST_STRIPE], U16, name="offsets")
 
         x_raw = [keep.tile([P, 2, T], F32, name=f"x_raw{u}") for u in range(2)]
-        x_bf = keep.tile([P, T, J], BF16, name="x_bf", align_bytes=64)
+        x_bf = keep.tile([P, T, PACK], BF16, name="x_bf", align_bytes=64)
         x_codes = keep.tile([P, T], U32, name="x_codes", align_bytes=64)
         x_scales = keep.tile([P, T], U8, name="x_scales", align_bytes=64)
-        g_codes = keep.tile([P, T], U32, name="g_codes", align_bytes=64)
-        g_scales = keep.tile([P, T], U8, name="g_scales", align_bytes=64)
-        w_raw = [keep.tile([P, J, N], F32, name=f"w_raw{d}") for d in range(D - 1)]
-        w_last = [keep.tile([P, J, P], F32, name=f"w_last{m}") for m in range(MB)]
-        w_bf = [keep.tile([P, D, P, J], BF16, name=f"w_bf{m}", align_bytes=64) for m in range(MB)]
-        w_codes = [keep.tile([P, D, P], U32, name=f"w_codes{m}", align_bytes=64) for m in range(MB)]
-        w_scales = [keep.tile([P, D, P], U8, name=f"w_scales{m}", align_bytes=64) for m in range(MB)]
-        bias = keep.tile([P, MB], F32, name="bias")
-        gates = [keep.tile([P, T], F32, name=f"gates{m}") for m in range(MB)]
-        y = [keep.tile([P, 2 * V], F32, name=f"y{m}") for m in range(MB)]
-        spread = [keep.tile([P, T], F32, name=f"spread{m}") for m in range(MB)]
+        picked_codes = keep.tile([P, T], U32, name="picked_codes", tag="codes_then_y", align_bytes=64)
+        picked_scales = keep.tile([P, T], U8, name="picked_scales", align_bytes=64)
+
+        w_raw = [keep.tile([P, PACK, N], F32, name=f"w_raw{d}") for d in range(D - 1)]
+        w_last = [keep.tile([P, PACK, P], F32, name=f"w_last{m}") for m in range(BLOCKS)]
+        w_bf = [keep.tile([P, D, P, PACK], BF16, name=f"w_bf{m}", align_bytes=64) for m in range(BLOCKS)]
+        w_codes = [keep.tile([P, D, P], U32, name=f"w_codes{m}", align_bytes=64) for m in range(BLOCKS)]
+        w_scales = [keep.tile([P, D, P], U8, name=f"w_scales{m}", align_bytes=64) for m in range(BLOCKS)]
+
+        bias = keep.tile([P, BLOCKS], F32, name="bias")
+        gates = [keep.tile([P, T], F32, name=f"gates{m}") for m in range(BLOCKS)]
+        y = [keep.tile([P, 2 * V], F32, name=f"y{m}", align_bytes=64) for m in range(BLOCKS)]
+        spread = [keep.tile([P, T], F32, name=f"spread{m}") for m in range(BLOCKS)]
         warm = keep.tile([P, 2], F32, name="warm")
-        acc = [psum.tile([P, V], F32, name=f"acc{m}") for m in range(MB)]
+        acc = [psum.tile([P, V], F32, name=f"acc{m}") for m in range(BLOCKS)]
 
         nc.gpsimd.memset(warm[:, 0:1], 0.0)
         nc.scalar.activation(warm[:, 1:2], warm[:, 0:1], RELU)
         nc.gpsimd.memset(x_scales[:], 0)
 
-        x_view = xT.rearrange("(p j) t -> p j t", j=J)
-
-
-        def group(engine_copy, dst, src):
-            engine_copy(
-                out=dst.rearrange("p (c i) t -> p c t i", i=4),
-                in_=src.rearrange("p t (c i) -> p c t i", i=4),
-            )
-
+        x_view = xT.rearrange("(p j) t -> p j t", j=PACK)
         nc.sync.dma_start(out=x_raw[0][:], in_=x_view[:, 0:2, :])
         nc.sync.dma_start(out=x_raw[1][:], in_=x_view[:, 2:4, :])
         nc.sync.dma_start(offsets[:], offs)
         for d in range(D):
-            w_view = w[d].rearrange("(p j) n -> p j n", j=J)
+            w_view = w[d].rearrange("(p j) n -> p j n", j=PACK)
             if d < D - 1:
                 nc.sync.dma_start(out=w_raw[d][:], in_=w_view)
             else:
-                for m in range(MB):
-                    cols = slice(m * P, (m + 1) * P)
-                    nc.sync.dma_start(out=w_last[m][:], in_=w_view[:, :, cols])
+                for m in range(BLOCKS):
+                    nc.sync.dma_start(out=w_last[m][:], in_=w_view[:, :, m * P : (m + 1) * P])
         nc.sync.dma_start(out=bias[:], in_=b.rearrange("(m p) o -> p (m o)", p=P))
-        nc.sync.dma_start(out=gates[0][:], in_=gate[0:P, :])
-        nc.sync.dma_start(out=gates[1][:], in_=gate[P : 2 * P, :])
+        for m in range(BLOCKS):
+            nc.sync.dma_start(out=gates[m][:], in_=gate[m * P : (m + 1) * P, :])
 
-        for u in range(2):
-            pair = slice(2 * u, 2 * u + 2)
-            group(nc.vector.tensor_copy, x_bf[:, 0:XV, pair], x_raw[u][:, :, 0:XV])
-            group(nc.scalar.copy, x_bf[:, XV:T, pair], x_raw[u][:, :, XV:T])
-        for h in range(2):
-            cols = slice(h * 256, (h + 1) * 256)
-            nc.vector.quantize_mx(
-                out=x_codes[:, cols].bitcast(FP8X4),
-                scales=x_scales[:, cols],
-                in_=x_bf[:, cols, :].rearrange("p t j -> p (t j)"),
+        def interleave(engine_copy, dst, src):
+            engine_copy(
+                dst.rearrange("p (c i) t -> p c t i", i=RUN),
+                src.rearrange("p t (c i) -> p c t i", i=RUN),
             )
 
-        def gather(dst, src, h):
-            nc.vector.tensor_copy(dst[:, h * 256 : (h + 1) * 256], src[:].indirect(offsets[:, h * 16 : (h + 1) * 16]))
+        def gpsimd_copy(dst, src):
+            nc.gpsimd.tensor_scalar(dst, src, 1.0, 0.0, MULT, ADD)
 
-        def quantize_w(m, a, e):
+        def interleave_w(engine_copy, m, d):
+            raw = w_raw[d][:, :, m * P : (m + 1) * P] if d < D - 1 else w_last[m][:]
+            interleave(engine_copy, w_bf[m][:, d, :, :], raw)
+
+        def quantize_w(m, first, end):
             nc.vector.quantize_mx(
-                out=w_codes[m][:, a:e, :].rearrange("p d n -> p (d n)").bitcast(FP8X4),
-                scales=w_scales[m][:, a:e, :].rearrange("p d n -> p (d n)"),
-                in_=w_bf[m][:, a:e, :, :].rearrange("p d n j -> p (d n j)"),
+                out=w_codes[m][:, first:end, :].rearrange("p d n -> p (d n)").bitcast(FP8X4),
+                scales=w_scales[m][:, first:end, :].rearrange("p d n -> p (d n)"),
+                in_=w_bf[m][:, first:end, :, :].rearrange("p d n j -> p (d n j)"),
             )
+
+        def list_slice(first, end):
+            return offsets[:, first * V // LIST_STRIPE : end * V // LIST_STRIPE]
+
+        def gather(dst, src, first, end):
+            nc.vector.tensor_copy(dst[:, first * V : end * V], src[:].indirect(list_slice(first, end)))
 
         def multiply(m, d):
+            members = slice(d * V, (d + 1) * V)
             nc.tensor.matmul_mx(
                 out=acc[m][:],
                 lhsT=w_codes[m][:, d, :].bitcast(FP8X4),
                 lhsT_scale=w_scales[m][:, d, :],
-                rhs=g_codes[:, d * V : (d + 1) * V].bitcast(FP8X4),
-                rhs_scale=g_scales[:, d * V : (d + 1) * V],
+                rhs=picked_codes[:, members].bitcast(FP8X4),
+                rhs_scale=picked_scales[:, members],
                 start=(d == 0),
                 stop=(d == D - 1),
             )
 
-        def finish(m, r):
-            nc.scalar.activation(y[m][:, r * V : (r + 1) * V], acc[m][:], RELU, bias=bias[:, m : m + 1])
+        def finish(m, pair):
+            nc.scalar.activation(
+                pair[:].rearrange("p (r v) -> p r v", r=2),
+                acc[m][:].unsqueeze(1).to_broadcast([P, 2, V]),
+                RELU,
+                bias=bias[:, m : m + 1],
+            )
 
-        def scatter(m, a, e):
+        def scatter(m, pair, first, end):
             nc.vector.tensor_tensor(
-                spread[m][:].indirect(offsets[:, a * 8 : e * 8]),
-                y[m][:, 0 : (e - a) * V],
-                gates[m][:, a * V : e * V],
+                spread[m][:].indirect(list_slice(first, end)),
+                pair[:],
+                gates[m][:, first * V : end * V],
                 MULT,
             )
 
-        def copy_w(engine_copy, m, d):
-            raw = w_raw[d][:, :, m * P : (m + 1) * P] if d < D - 1 else w_last[m][:]
-            group(engine_copy, w_bf[m][:, d, :, :], raw)
-
-        def copy_gpsimd(out, in_):
-            nc.gpsimd.tensor_scalar(out, in_, 1.0, 0.0, MULT, ADD)
+        for u in range(2):
+            rows = slice(2 * u, 2 * u + 2)
+            interleave(nc.vector.tensor_copy, x_bf[:, 0:X_SPLIT, rows], x_raw[u][:, :, 0:X_SPLIT])
+            interleave(nc.scalar.copy, x_bf[:, X_SPLIT:T, rows], x_raw[u][:, :, X_SPLIT:T])
+        for h in range(T // HALF):
+            tokens = slice(h * HALF, (h + 1) * HALF)
+            nc.vector.quantize_mx(
+                out=x_codes[:, tokens].bitcast(FP8X4),
+                scales=x_scales[:, tokens],
+                in_=x_bf[:, tokens, :].rearrange("p t j -> p (t j)"),
+            )
 
         for d in range(2):
-            copy_w(nc.scalar.copy, 0, d)
-            copy_w(copy_gpsimd, 1, d)
-        copy_w(nc.scalar.copy, 0, 2)
-        copy_w(nc.scalar.copy, 1, 2)
-        gather(g_codes, x_codes, 0)
-        gather(g_scales, x_scales, 0)
-        gather(g_codes, x_codes, 1)
+            interleave_w(nc.scalar.copy, 0, d)
+            interleave_w(gpsimd_copy, 1, d)
+        interleave_w(nc.scalar.copy, 0, 2)
+        interleave_w(nc.scalar.copy, 1, 2)
+
+        gather(picked_codes, x_codes, 0, 2)
+        gather(picked_scales, x_scales, 0, 2)
+        gather(picked_codes, x_codes, 2, 4)
         quantize_w(0, 0, 2)
         multiply(0, 0)
         multiply(0, 1)
-        gather(g_scales, x_scales, 1)
-        copy_w(nc.vector.tensor_copy, 0, 3)
+        gather(picked_scales, x_scales, 2, 4)
+        interleave_w(nc.vector.tensor_copy, 0, 3)
         quantize_w(0, 2, 3)
         multiply(0, 2)
-        copy_w(nc.scalar.copy, 1, 3)
+        interleave_w(nc.scalar.copy, 1, 3)
         quantize_w(0, 3, 4)
         multiply(0, 3)
-        finish(0, 0)
-        finish(0, 1)
+        finish(0, y[0])
+
         quantize_w(1, 0, 2)
         quantize_w(1, 2, 4)
-        scatter(0, 0, 1)
-        scatter(0, 1, 3)
+        scatter(0, y[0], 0, 2)
         for d in range(D):
             multiply(1, d)
-        finish(1, 0)
-        finish(1, 1)
-        scatter(1, 0, 2)
-        scatter(0, 3, 4)
+        finish(1, y[1])
+
+        y_late = keep.tile([P, 2 * V], F32, name="y_late", tag="codes_then_y", align_bytes=64)
+        finish(0, y_late)
+        scatter(1, y[1], 0, 2)
+        scatter(0, y_late, 2, 4)
         nc.sync.dma_start(out=out[0:P, :], in_=spread[0][:])
-        scatter(1, 2, 4)
+        scatter(1, y[1], 2, 4)
         nc.sync.dma_start(out=out[P : 2 * P, :], in_=spread[1][:])

from contextlib import ExitStack

import concourse.mybir as mybir

K, T, D, V, N = 512, 512, 4, 128, 256
P = 128
PACK = 4
BLOCKS = N // P
HALF = T // 2
LIST_STRIPE = 16
RUN = 4

X_SPLIT = 320

FLOPS = 2 * D * K * V * N

F32 = mybir.dt.float32
BF16 = mybir.dt.bfloat16
U32 = mybir.dt.uint32
U16 = mybir.dt.uint16
U8 = mybir.dt.uint8
FP8X4 = mybir.dt.float8_e4m3fn_x4
RELU = mybir.ActivationFunctionType.Relu
MULT = mybir.AluOpType.mult
ADD = mybir.AluOpType.add


def tile_picked_tome_lin_relu_sub_e_kernel(tc, xT, w, b, gate, offs, out):
    nc = tc.nc
    with ExitStack() as ctx:
        lists = ctx.enter_context(tc.tile_pool(name="lists", bufs=1))
        keep = ctx.enter_context(tc.tile_pool(name="keep", bufs=1))
        psum = ctx.enter_context(tc.psum_pool(name="psum", bufs=1))

        offsets = lists.tile([P, T // LIST_STRIPE], U16, name="offsets")

        x_raw = [keep.tile([P, 2, T], F32, name=f"x_raw{u}") for u in range(2)]
        x_bf = keep.tile([P, T, PACK], BF16, name="x_bf", align_bytes=64)
        x_codes = keep.tile([P, T], U32, name="x_codes", align_bytes=64)
        x_scales = keep.tile([P, T], U8, name="x_scales", align_bytes=64)
        picked_codes = keep.tile([P, T], U32, name="picked_codes", tag="codes_then_y", align_bytes=64)
        picked_scales = keep.tile([P, T], U8, name="picked_scales", align_bytes=64)

        w_raw = [keep.tile([P, PACK, N], F32, name=f"w_raw{d}") for d in range(D - 1)]
        w_last = [keep.tile([P, PACK, P], F32, name=f"w_last{m}") for m in range(BLOCKS)]
        w_bf = [keep.tile([P, D, P, PACK], BF16, name=f"w_bf{m}", align_bytes=64) for m in range(BLOCKS)]
        w_codes = [keep.tile([P, D, P], U32, name=f"w_codes{m}", align_bytes=64) for m in range(BLOCKS)]
        w_scales = [keep.tile([P, D, P], U8, name=f"w_scales{m}", align_bytes=64) for m in range(BLOCKS)]

        bias = keep.tile([P, BLOCKS], F32, name="bias")
        gates = [keep.tile([P, T], F32, name=f"gates{m}") for m in range(BLOCKS)]
        y = [keep.tile([P, 2 * V], F32, name=f"y{m}", align_bytes=64) for m in range(BLOCKS)]
        spread = [keep.tile([P, T], F32, name=f"spread{m}") for m in range(BLOCKS)]
        warm = keep.tile([P, 2], F32, name="warm")
        acc = [psum.tile([P, V], F32, name=f"acc{m}") for m in range(BLOCKS)]

        nc.gpsimd.memset(warm[:, 0:1], 0.0)
        nc.scalar.activation(warm[:, 1:2], warm[:, 0:1], RELU)
        nc.gpsimd.memset(x_scales[:], 0)

        x_view = xT.rearrange("(p j) t -> p j t", j=PACK)
        nc.sync.dma_start(out=x_raw[0][:], in_=x_view[:, 0:2, :])
        nc.sync.dma_start(out=x_raw[1][:], in_=x_view[:, 2:4, :])
        nc.sync.dma_start(offsets[:], offs)
        for d in range(D):
            w_view = w[d].rearrange("(p j) n -> p j n", j=PACK)
            if d < D - 1:
                nc.sync.dma_start(out=w_raw[d][:], in_=w_view)
            else:
                for m in range(BLOCKS):
                    nc.sync.dma_start(out=w_last[m][:], in_=w_view[:, :, m * P : (m + 1) * P])
        nc.sync.dma_start(out=bias[:], in_=b.rearrange("(m p) o -> p (m o)", p=P))
        for m in range(BLOCKS):
            nc.sync.dma_start(out=gates[m][:], in_=gate[m * P : (m + 1) * P, :])

        def interleave(engine_copy, dst, src):
            engine_copy(
                dst.rearrange("p (c i) t -> p c t i", i=RUN),
                src.rearrange("p t (c i) -> p c t i", i=RUN),
            )

        def gpsimd_copy(dst, src):
            nc.gpsimd.tensor_scalar(dst, src, 1.0, 0.0, MULT, ADD)

        def interleave_w(engine_copy, m, d):
            raw = w_raw[d][:, :, m * P : (m + 1) * P] if d < D - 1 else w_last[m][:]
            interleave(engine_copy, w_bf[m][:, d, :, :], raw)

        def quantize_w(m, first, end):
            nc.vector.quantize_mx(
                out=w_codes[m][:, first:end, :].rearrange("p d n -> p (d n)").bitcast(FP8X4),
                scales=w_scales[m][:, first:end, :].rearrange("p d n -> p (d n)"),
                in_=w_bf[m][:, first:end, :, :].rearrange("p d n j -> p (d n j)"),
            )

        def list_slice(first, end):
            return offsets[:, first * V // LIST_STRIPE : end * V // LIST_STRIPE]

        def gather(dst, src, first, end):
            nc.vector.tensor_copy(dst[:, first * V : end * V], src[:].indirect(list_slice(first, end)))

        def multiply(m, d):
            members = slice(d * V, (d + 1) * V)
            nc.tensor.matmul_mx(
                out=acc[m][:],
                lhsT=w_codes[m][:, d, :].bitcast(FP8X4),
                lhsT_scale=w_scales[m][:, d, :],
                rhs=picked_codes[:, members].bitcast(FP8X4),
                rhs_scale=picked_scales[:, members],
                start=(d == 0),
                stop=(d == D - 1),
            )

        def finish(m, pair):
            nc.scalar.activation(
                pair[:].rearrange("p (r v) -> p r v", r=2),
                acc[m][:].unsqueeze(1).to_broadcast([P, 2, V]),
                RELU,
                bias=bias[:, m : m + 1],
            )

        def scatter(m, pair, first, end):
            nc.vector.tensor_tensor(
                spread[m][:].indirect(list_slice(first, end)),
                pair[:],
                gates[m][:, first * V : end * V],
                MULT,
            )

        for u in range(2):
            rows = slice(2 * u, 2 * u + 2)
            interleave(nc.vector.tensor_copy, x_bf[:, 0:X_SPLIT, rows], x_raw[u][:, :, 0:X_SPLIT])
            interleave(nc.scalar.copy, x_bf[:, X_SPLIT:T, rows], x_raw[u][:, :, X_SPLIT:T])
        for h in range(T // HALF):
            tokens = slice(h * HALF, (h + 1) * HALF)
            nc.vector.quantize_mx(
                out=x_codes[:, tokens].bitcast(FP8X4),
                scales=x_scales[:, tokens],
                in_=x_bf[:, tokens, :].rearrange("p t j -> p (t j)"),
            )

        for d in range(2):
            interleave_w(nc.scalar.copy, 0, d)
            interleave_w(gpsimd_copy, 1, d)
        interleave_w(nc.scalar.copy, 0, 2)
        interleave_w(nc.scalar.copy, 1, 2)

        gather(picked_codes, x_codes, 0, 2)
        gather(picked_scales, x_scales, 0, 2)
        gather(picked_codes, x_codes, 2, 4)
        quantize_w(0, 0, 2)
        multiply(0, 0)
        multiply(0, 1)
        gather(picked_scales, x_scales, 2, 4)
        interleave_w(nc.vector.tensor_copy, 0, 3)
        quantize_w(0, 2, 3)
        multiply(0, 2)
        interleave_w(nc.scalar.copy, 1, 3)
        quantize_w(0, 3, 4)
        multiply(0, 3)
        finish(0, y[0])

        quantize_w(1, 0, 2)
        quantize_w(1, 2, 4)
        scatter(0, y[0], 0, 2)
        for d in range(D):
            multiply(1, d)
        finish(1, y[1])

        y_late = keep.tile([P, 2 * V], F32, name="y_late", tag="codes_then_y", align_bytes=64)
        finish(0, y_late)
        scatter(1, y[1], 0, 2)
        scatter(0, y_late, 2, 4)
        nc.sync.dma_start(out=out[0:P, :], in_=spread[0][:])
        scatter(1, y[1], 2, 4)
        nc.sync.dma_start(out=out[P : 2 * P, :], in_=spread[1][:])
